import numpy as np
import ml_dtypes


def mxq(x, axis, fmt="e4m3"):
    dtype, down = {"e4m3": (ml_dtypes.float8_e4m3fn, 7), "e5m2": (ml_dtypes.float8_e5m2, 14)}[fmt]
    v = np.moveaxis(np.asarray(x, np.float32).astype(ml_dtypes.bfloat16).astype(np.float64), axis, -1)
    blocks = v.reshape(v.shape[:-1] + (-1, 32))
    amax = np.abs(blocks).max(-1, keepdims=True)
    byte = np.maximum(np.where(amax > 0, np.frexp(amax)[1] - 1 + 127, 0) - down, 1)
    scale = np.exp2(byte - 127.0)
    codes = (blocks / scale).astype(np.float32).astype(dtype).astype(np.float64)
    return np.moveaxis((codes * scale).reshape(v.shape), -1, axis)


WIDE = False


def mx_kscale(k):
    if not WIDE:
        return np.ones(k)
    levels = np.array([10, -10, 5, -5, 0])
    if k % 512:
        return np.exp2(np.random.permutation(np.resize(levels, k // 32))).repeat(32)
    a = np.empty((k // 512, 16))
    for p in range(k // 512):
        a[p, :8] = np.random.permutation(np.resize(levels, 8))
        for g in range(8):
            far = levels[np.abs(levels - a[p, g]) >= 10]
            a[p, g + 8] = far[np.random.randint(len(far))]
    return np.exp2(a.ravel()).repeat(32)


def f64(x):
    return np.asarray(x).astype(np.float64)


def striped(idx):
    return np.tile(idx.reshape(-1, 16).T, (8, 1)).astype(np.uint16)


def unstriped(offs):
    return offs[:16].T.reshape(-1).astype(np.int64)


E2M1 = np.array([0.0, 0.5, 1.0, 1.5, 2.0, 3.0, 4.0, 6.0, -0.0, -0.5, -1.0, -1.5, -2.0, -3.0, -4.0, -6.0])


def pack_weight(w, fmt):
    k, n = w.shape
    w = f64(np.asarray(w, np.float32).astype(ml_dtypes.bfloat16)).reshape(k // 32, 32, n)
    amax = np.abs(w).max(1)
    if fmt == "e4m3":
        byte = np.frexp(amax)[1] - 1 + 127 - 7
    else:
        mant, ex = np.frexp(amax / 6.0)
        byte = np.where(mant > 0.5, ex, ex - 1) + 127
    byte = np.clip(np.where(amax > 0, byte, 1), 1, 254)
    scaled = (w * np.exp2(127.0 - byte)[:, None, :]).reshape(k, n).astype(np.float32)
    by_word = np.ascontiguousarray(scaled.reshape(k // 512, 128, 4, n).transpose(0, 1, 3, 2))
    if fmt == "e4m3":
        words = by_word.astype(ml_dtypes.float8_e4m3fn).view(np.uint8)
    else:
        c = by_word.astype(ml_dtypes.float4_e2m1fn).view(np.uint8) & 0xF
        words = (c[..., 0::2] | (c[..., 1::2] << 4)).reshape(k // 512, 128, 2 * n)
    return np.ascontiguousarray(words), np.ascontiguousarray(byte.astype(np.uint8).reshape(k // 512, 16, n))


def unpack_weight(words, scales, fmt):
    g, _, n = scales.shape
    words = np.ascontiguousarray(words).reshape(g, 128, n, -1)
    if fmt == "e4m3":
        vals = words.view(ml_dtypes.float8_e4m3fn).astype(np.float64)
    else:
        nib = np.empty((g, 128, n, 4), np.uint8)
        nib[..., 0::2] = words & 0xF
        nib[..., 1::2] = words >> 4
        vals = E2M1[nib]
    vals = vals * np.repeat(np.exp2(scales.astype(np.float64) - 127.0), 8, axis=1)[..., None]
    return vals.transpose(0, 1, 3, 2).reshape(g * 512, n)


def gelu(v):
    return 0.5 * v * (1.0 + np.tanh(np.sqrt(2.0 / np.pi) * (v + 0.044715 * v**3)))


def bf(x):
    return np.asarray(x, np.float32).astype(ml_dtypes.bfloat16)


def planes(Y):
    n, m = Y.shape
    b = f64(bf(Y)).reshape(n // 32, 32, m)
    amax = np.abs(b).max(1)
    byte = np.clip(np.where(amax > 0, np.frexp(amax)[1] - 1 + 127 - 7, 1), 1, 254)
    codes = (b * np.exp2(127.0 - byte)[:, None, :]).reshape(n, m).astype(np.float32).astype(ml_dtypes.float8_e4m3fn).view(np.uint8)
    words = codes.reshape(n // 512, 128, 4, m).transpose(0, 1, 3, 2)
    return np.ascontiguousarray(words), np.ascontiguousarray(byte.astype(np.uint8).reshape(n // 512, 16, m))


K, H, N, T, S, P = 1024, 512, 1024, 4096, 1024, 512

def setup_inputs():
    n = np.random.standard_normal
    s = mx_kscale(K)[:, None]
    u = mx_kscale(H)[:, None]
    tab_words, tab_scales = pack_weight(n((K, T)) * s, "e4m3")
    w1 = n((K, H)) / np.sqrt(K) / s
    w2_words, w2_scales = pack_weight(0.52 * n((K, H)) / np.sqrt(K) / s, "e4m3")
    w3_words, w3_scales = pack_weight(0.7 * n((K, H)) / np.sqrt(K) / s, "e2m1")
    size = np.exp(0.8 * n(N))
    wa = n((H, N)) / np.sqrt(H) / u * size[None, :]
    wb_words, wb_scales = pack_weight(n((H, N)) / np.sqrt(H) / u * size[None, :], "e2m1")
    return {
        "tab_words": tab_words, "tab_scales": tab_scales,
        "offs": striped(np.random.permutation(T)[:S]),
        "w1": w1.astype(np.float32),
        "w2_words": w2_words, "w2_scales": w2_scales,
        "w3_words": w3_words, "w3_scales": w3_scales,
        "gain": (np.exp(0.3 * n(H)) * u[:, 0]).astype(np.float32),
        "pos1": striped(np.random.permutation(S)[:P]),
        "pos2": striped(np.random.permutation(S)[:P]),
        "vd": np.exp(0.4 * n(H)).astype(np.float32),
        "ga": n((H, P)).astype(np.float32),
        "wa": wa.astype(np.float32),
        "wb_words": wb_words, "wb_scales": wb_scales,
        "res": (0.7 * n((N, P)) * size[:, None]).astype(np.float32),
    }

def reference(tab_words, tab_scales, offs, w1, w2_words, w2_scales, w3_words, w3_scales, gain, pos1, pos2, vd, ga, wa, wb_words, wb_scales, res):
    v = unpack_weight(tab_words, tab_scales, "e4m3")[:, unstriped(offs)]
    a = mxq(f64(w1), 0, "e4m3").T @ v
    b = unpack_weight(w2_words, w2_scales, "e4m3").T @ v
    d = unpack_weight(w3_words, w3_scales, "e2m1").T @ v
    h = np.maximum(a * np.cos(b), d) * f64(gain)[:, None]
    xa = h[:, unstriped(pos1)] * f64(vd)[:, None]
    xb = h[:, unstriped(pos2)] * f64(ga)
    ya = mxq(f64(wa), 0, "e4m3").T @ mxq(xa, 0, "e4m3")
    yb = unpack_weight(wb_words, wb_scales, "e2m1").T @ mxq(xb, 0, "e4m3")
    y = (ya + yb) + f64(res)
    words, scales = planes(y)
    return y, words, scales

@@ -1,0 +1,294 @@
+from contextlib import ExitStack
+import math
+
+import concourse.mybir as mybir
+
+K, H, N, T, S, P = 1024, 512, 1024, 4096, 1024, 512
+FLOPS = 2 * (3 * K * H * S + 2 * H * N * P)
+
+F32 = mybir.dt.float32
+BF16 = mybir.dt.bfloat16
+I32 = mybir.dt.int32
+U32 = mybir.dt.uint32
+U16 = mybir.dt.uint16
+U8 = mybir.dt.uint8
+FP8X4 = mybir.dt.float8_e4m3fn_x4
+FP4X4 = mybir.dt.float4_e2m1fn_x4
+ALU = mybir.AluOpType
+ACT = mybir.ActivationFunctionType
+
+PARTS = 128
+BANK = 512
+MH = 2
+MW = P // MH
+
+
+def tile_list_bladder_pressure_reading_kernel(
+    tc, tab_words, tab_scales, offs, w1, w2_words, w2_scales, w3_words, w3_scales, gain, pos1, pos2, vd, ga, wa,
+    wb_words, wb_scales, res, out_0, out_1, out_2,
+):
+    nc = tc.nc
+    with ExitStack() as ctx:
+        lists = ctx.enter_context(tc.tile_pool(name="lists", bufs=1))
+        keep = ctx.enter_context(tc.tile_pool(name="keep", bufs=1))
+        ring = ctx.enter_context(tc.tile_pool(name="ring", bufs=2))
+        psum = ctx.enter_context(tc.psum_pool(name="psum", bufs=1))
+
+        def kt(shape, dt, name, tag=""):
+            return keep.tile(shape, dt, name=name, tag=tag or name, align_bytes=64)
+
+        offs_t = lists.tile([PARTS, S // 16], U16, name="offs_t")
+        pos1_t = lists.tile([PARTS, P // 16], U16, name="pos1_t")
+        pos2_t = lists.tile([PARTS, P // 16], U16, name="pos2_t")
+
+        tab_sc = kt([PARTS, T], U8, "tab_sc")
+        w23_sc_raw = kt([PARTS, 2, H], U8, "w23_sc_raw")
+        wb_sc_raw = kt([PARTS, 2, 512], U8, "wb_sc_raw")
+        v_sc1 = kt([PARTS, S], U8, "v_sc1")
+        nc.vector.memset(tab_sc[:].bitcast(I32), 0)
+        nc.vector.memset(w23_sc_raw[:].bitcast(I32), 0)
+        nc.vector.memset(v_sc1[:].bitcast(I32), 0)
+
+        tab_w = [kt([PARTS, T], U32, "tab_w%d" % a) for a in range(2)]
+        w1_raw = [kt([PARTS, 4, H], F32, "w1_raw%d" % a) for a in range(2)]
+        w2_raw = kt([PARTS, 2, H], I32, "w2_raw")
+        w3_raw = kt([PARTS, 2, H], U16, "w3_raw")
+        gain_t = kt([PARTS, 4], F32, "gain_t")
+        vd_t = kt([PARTS, 4], F32, "vd_t")
+        w23_sc_in = kt([PARTS, 2, H // 4], I32, "w23_sc_in")
+
+        def load_tab(a):
+            nc.sync.dma_start(out=tab_w[a][:].bitcast(I32), in_=tab_words[a].rearrange("p n t -> p (n t)").bitcast(I32))
+
+        def load_w1(a):
+            nc.sync.dma_start(out=w1_raw[a][:], in_=w1[512 * a : 512 * (a + 1), :].rearrange("(p i) c -> p i c", i=4))
+
+        def load_w_scales(src, row0):
+            for q in range(4):
+                nc.sync.dma_start(
+                    out=w23_sc_in[32 * q + row0 : 32 * q + row0 + 4, :, :],
+                    in_=src[:, 4 * q : 4 * q + 4, :].rearrange("a r c -> r a c").bitcast(I32),
+                )
+
+        wb_raw = kt([PARTS, 2, 512], U16, "wb_raw")
+        nc.gpsimd.memset(wb_sc_raw[:].bitcast(I32), 0)
+        for q in range(4):
+            nc.gpsimd.dma_start(
+                out=wb_sc_raw[32 * q : 32 * q + 4, :, :].rearrange("p g c -> p (g c)").bitcast(I32),
+                in_=wb_scales[0, 4 * q : 4 * q + 4, :].bitcast(I32),
+            )
+        nc.sync.dma_start(offs_t[:], offs)
+        tab_sc_in = kt([PARTS, T // 4], I32, "tab_sc_in")
+        for q in range(4):
+            nc.sync.dma_start(out=tab_sc_in[32 * q : 32 * q + 8, :], in_=tab_scales[:, 4 * q : 4 * q + 4, :].bitcast(I32))
+        nc.sync.dma_start(out=w3_raw[:].bitcast(I32), in_=w3_words.rearrange("a p c -> p a c").bitcast(I32))
+        nc.sync.dma_start(out=w2_raw[:], in_=w2_words.rearrange("a p c i -> p a (c i)").bitcast(I32))
+        load_w1(0)
+        load_w_scales(w2_scales, 4)
+        nc.sync.dma_start(out=wb_raw[:].rearrange("p g c -> p (g c)").bitcast(I32), in_=wb_words[0].bitcast(I32))
+        load_tab(0)
+        load_w_scales(w3_scales, 0)
+        nc.sync.dma_start(out=gain_t[:], in_=gain.rearrange("(p t) -> p t", t=4))
+        nc.sync.dma_start(out=vd_t[:], in_=vd.rearrange("(p t) -> p t", t=4))
+        load_tab(1)
+        load_w1(1)
+        nc.sync.dma_start(pos1_t[:], pos1)
+        nc.sync.dma_start(pos2_t[:], pos2)
+
+        v_sc = kt([PARTS, S], U8, "v_sc")
+        for q in range(4):
+            rows = slice(32 * q, 32 * q + 8)
+            nc.vector.tensor_copy(tab_sc[rows, :].bitcast(I32), tab_sc_in[rows, :])
+        nc.vector.tensor_copy(v_sc[:], tab_sc[:].indirect(offs_t[:]))
+        for q in range(4):
+            nc.sync.dma_start(
+                out=v_sc1[32 * q : 32 * q + 4, :].bitcast(I32), in_=v_sc[32 * q + 4 : 32 * q + 8, :].bitcast(I32)
+            )
+        ga_t = kt([PARTS, 4, P], F32, "ga_t", "tab_sc")
+        nc.sync.dma_start(out=ga_t[:], in_=ga.rearrange("(p t) m -> p t m", t=4))
+        v_w = [[kt([PARTS, BANK], U32, "v_w%d_%d" % (a, jh)) for jh in range(2)] for a in range(2)]
+
+        def gather_tab(a):
+            for jh in range(2):
+                nc.vector.tensor_copy(v_w[a][jh][:], tab_w[a][:].indirect(offs_t[:, 32 * jh : 32 * (jh + 1)]))
+
+        def deal(dst, src):
+            nc.vector.tensor_copy(
+                out=dst.rearrange("p a (t m) -> p a m t", t=4), in_=src.rearrange("p a (m t) -> p a m t", t=4)
+            )
+
+        def round_weight(eng, raw, name, tag):
+            wbf = kt([PARTS, 4, PARTS, 4], BF16, name, tag)
+            o = wbf[:].rearrange("p t m i -> p m i t")
+            s = raw[:].rearrange("p i (m t) -> p m i t", t=4)
+            if eng == "scalar":
+                nc.scalar.copy(out=o, in_=s)
+            else:
+                nc.vector.tensor_copy(out=o, in_=s)
+            return wbf
+
+        def quantize(codes, scales, src):
+            nc.vector.quantize_mx(out=codes.bitcast(FP8X4), scales=scales, in_=src)
+
+        w2_c = kt([PARTS, 2, H], U32, "w2_c")
+        w3_c = kt([PARTS, 2, H], U16, "w3_c")
+        w23_sc = kt([PARTS, 2, H], U8, "w23_sc")
+        deal(w2_c[:].bitcast(I32), w2_raw[:])
+        deal(w3_c[:], w3_raw[:])
+        wb_c = kt([PARTS, 2, 512], U16, "wb_c")
+        deal(wb_c[:], wb_raw[:])
+        w1_c = [kt([PARTS, H], U32, "w1_c%d" % a) for a in range(2)]
+        w1_sc = [kt([PARTS, H], U8, "w1_sc%d" % a) for a in range(2)]
+        wbf = round_weight("scalar", w1_raw[0], "w1bf0", "")
+        quantize(w1_c[0][:], w1_sc[0][:], wbf[:].rearrange("p t m i -> p (t m i)"))
+        gather_tab(0)
+        for q in range(4):
+            rows = slice(32 * q, 32 * q + 8)
+            nc.vector.tensor_copy(w23_sc_raw[rows, :, :].bitcast(I32), w23_sc_in[rows, :, :])
+        deal(w23_sc[:], w23_sc_raw[:])
+        gather_tab(1)
+        wbf = round_weight("vector", w1_raw[1], "w1bf1", "tab_w1")
+        quantize(w1_c[1][:], w1_sc[1][:], wbf[:].rearrange("p t m i -> p (t m i)"))
+
+        wa_both = kt([PARTS, 2, 4, 512], F32, "wa_both", "tab_w0")
+        wa_raw = [wa_both[:, g] for g in range(2)]
+        for g in range(2):
+            nc.sync.dma_start(out=wa_raw[g][:], in_=wa[:, 512 * g : 512 * (g + 1)].rearrange("(p i) c -> p i c", i=4))
+        res_v = res.rearrange("(g p t) m -> g p t m", g=2, t=4)
+        y = []
+
+        def load_res(mh, tag):
+            y.append(kt([PARTS, 2, 4, MW], F32, "y%d" % mh, tag))
+            for g in range(2):
+                nc.sync.dma_start(out=y[mh][:, g], in_=res_v[g, :, :, MW * mh : MW * (mh + 1)])
+
+        load_res(0, "tab_w1")
+
+        gv = kt([PARTS, 4], F32, "gv")
+        nc.gpsimd.tensor_tensor(gv[:], gain_t[:], vd_t[:], ALU.mult)
+        gv_wide = kt([PARTS, 4, MW], F32, "gv_wide", "w1_raw0")
+        nc.scalar.copy(out=gv_wide[:], in_=gv[:].unsqueeze(2).to_broadcast([PARTS, 4, MW]))
+        gag = kt([PARTS, 4, P], F32, "gag", "w1_raw1")
+        for t in range(4):
+            nc.gpsimd.tensor_scalar(gag[:, t, :], ga_t[:, t, :], gain_t[:, t : t + 1], 0.0, ALU.mult, ALU.add)
+
+        h = [kt([PARTS, S], F32, "h%d" % t) for t in range(4)]
+        wa_c = [kt([PARTS, 512], U32, "wa_c%d" % g) for g in range(2)]
+        wa_sc = [kt([PARTS, 512], U8, "wa_sc%d" % g) for g in range(2)]
+
+        def products(t, jh):
+            cols = slice(PARTS * t, PARTS * (t + 1))
+            js = slice(BANK * jh, BANK * (jh + 1))
+            pb = psum.tile([PARTS, BANK], F32, name="pb", tag="pb", bufs=2)
+            pa = psum.tile([PARTS, BANK], F32, name="pa", tag="pa", bufs=3)
+            pd = psum.tile([PARTS, BANK], F32, name="pd", tag="pd", bufs=3)
+            for a in range(2):
+                nc.tensor.matmul_mx(
+                    out=pb[:], lhsT=w2_c[:, a, cols].bitcast(FP8X4), lhsT_scale=w23_sc[4:, a, cols],
+                    rhs=v_w[a][jh][:].bitcast(FP8X4), rhs_scale=v_sc[4 * a :, js], start=a == 0, stop=a == 1,
+                )
+            for a in range(2):
+                nc.tensor.matmul_mx(
+                    out=pa[:], lhsT=w1_c[a][:, cols].bitcast(FP8X4), lhsT_scale=w1_sc[a][:, cols],
+                    rhs=v_w[a][jh][:].bitcast(FP8X4), rhs_scale=v_sc[4 * a :, js], start=a == 0, stop=a == 1,
+                )
+            for a in range(2):
+                nc.tensor.matmul_mx(
+                    out=pd[:], lhsT=w3_c[:, a, cols].bitcast(FP4X4), lhsT_scale=w23_sc[:, a, cols],
+                    rhs=v_w[a][jh][:].bitcast(FP8X4), rhs_scale=(v_sc, v_sc1)[a][:, js], start=a == 0, stop=a == 1,
+                )
+            mag = ring.tile([PARTS, BANK], F32, name="mag")
+            cosb = kt([PARTS, BANK], F32, "cos%d_%d" % (t, jh))
+            nc.scalar.activation(mag[:], pb[:], ACT.Abs)
+            nc.scalar.activation(cosb[:], mag[:], ACT.Sin, bias=math.pi / 2, scale=-1.0)
+            return pa, pd, cosb
+
+        def slice_of_h(t):
+            parts = [products(t, jh) for jh in range(2)]
+            prods = []
+            for pa, pd, cosb in parts:
+                prod = ring.tile([PARTS, BANK], F32, name="prod")
+                nc.vector.tensor_tensor(prod[:], pa[:], cosb[:], ALU.mult)
+                prods.append(prod)
+            for jh in range(2):
+                nc.vector.tensor_tensor(h[t][:, BANK * jh : BANK * (jh + 1)], parts[jh][1][:], prods[jh][:], ALU.max)
+
+        def pick(t, mh, xa_g, xb_g):
+            ms = slice(MW * mh, MW * (mh + 1))
+            lo, hi = ms.start // 16, ms.stop // 16
+            nc.vector.tensor_tensor(xa_g[:, t, :], h[t][:].indirect(pos1_t[:, lo:hi]), gv_wide[:, t, :], ALU.mult)
+            nc.vector.tensor_tensor(xb_g[:, t, :], h[t][:].indirect(pos2_t[:, lo:hi]), gag[:, t, ms], ALU.mult)
+
+        def interleave(dst, src):
+            nc.scalar.copy(
+                out=dst.rearrange("p (c i) t -> p c t i", i=4), in_=src.rearrange("p t (c i) -> p c t i", i=4)
+            )
+
+        x_c, x_sc = {}, {}
+
+        def finish_x(mh, xa_g, xb_g):
+            for nm, src in (("a", xa_g), ("b", xb_g)):
+                xbf = kt([PARTS, MW, 4], BF16, "xbf%s%d" % (nm, mh))
+                interleave(xbf[:], src[:])
+                x_c[nm, mh] = kt([PARTS, MW], U32, "x_c%s%d" % (nm, mh))
+                x_sc[nm, mh] = kt([PARTS, MW], U8, "x_sc%s%d" % (nm, mh))
+                quantize(x_c[nm, mh][:], x_sc[nm, mh][:], xbf[:].rearrange("p m t -> p (m t)"))
+
+        xa_g = kt([PARTS, 4, MW], F32, "xa_g0")
+        xb_g = kt([PARTS, 4, MW], F32, "xb_g0")
+        for t in range(4):
+            slice_of_h(t)
+            pick(t, 0, xa_g, xb_g)
+            if t == 0:
+                load_res(1, "cos0_0")
+            if t == 1:
+                wb_sc = kt([PARTS, 2, 512], U8, "wb_sc", "cos1_0")
+                deal(wb_sc[:], wb_sc_raw[:])
+            if t in (1, 2):
+                g = t - 1
+                wbf = round_weight("scalar", wa_raw[g], "wabf%d" % g, "cos%d_1" % t)
+                quantize(wa_c[g][:], wa_sc[g][:], wbf[:].rearrange("p t m i -> p (t m i)"))
+        finish_x(0, xa_g, xb_g)
+        xa_g = kt([PARTS, 4, MW], F32, "xa_g1", "cos3_0")
+        xb_g = kt([PARTS, 4, MW], F32, "xb_g1", "cos3_1")
+        for t in range(4):
+            pick(t, 1, xa_g, xb_g)
+        finish_x(1, xa_g, xb_g)
+
+        y_c = [kt([PARTS, 2, MW], U32, "y_c%d" % mh) for mh in range(MH)]
+        y_sc = kt([PARTS, 2, P], U8, "y_sc")
+        out_y = out_0.rearrange("(g p t) m -> g p t m", g=2, t=4)
+        per_bank = BANK // MW
+        n_bank = 0
+        for mh in range(MH):
+            ms = slice(MW * mh, MW * (mh + 1))
+            for g in range(2):
+                for t0 in range(0, 4, per_bank):
+                    tag, bufs = (("pb", 2), ("pa", 3), ("pd", 3))[n_bank % 3]
+                    n_bank = n_bank + 1
+                    py = psum.tile([PARTS, per_bank, MW], F32, name="py", tag=tag, bufs=bufs)
+                    for u in range(per_bank):
+                        cols = slice(PARTS * (t0 + u), PARTS * (t0 + u + 1))
+                        nc.tensor.matmul_mx(
+                            out=py[:, u, :], lhsT=wb_c[:, g, cols].bitcast(FP4X4), lhsT_scale=wb_sc[:, g, cols],
+                            rhs=x_c["b", mh][:].bitcast(FP8X4), rhs_scale=x_sc["b", mh][:], start=True, stop=False,
+                        )
+                        nc.tensor.matmul_mx(
+                            out=py[:, u, :], lhsT=wa_c[g][:, cols].bitcast(FP8X4), lhsT_scale=wa_sc[g][:, cols],
+                            rhs=x_c["a", mh][:].bitcast(FP8X4), rhs_scale=x_sc["a", mh][:], start=False, stop=True,
+                        )
+                    ts = slice(t0, t0 + per_bank)
+                    nc.vector.tensor_tensor(y[mh][:, g, ts, :], py[:], y[mh][:, g, ts, :], ALU.add)
+                nc.sync.dma_start(out=out_y[g, :, :, ms], in_=y[mh][:, g])
+                ybf = ring.tile([PARTS, MW, 4], BF16, name="ybf", align_bytes=64)
+                interleave(ybf[:], y[mh][:, g])
+                quantize(y_c[mh][:, g, :], y_sc[:, g, ms], ybf[:].rearrange("p m t -> p (m t)"))
+            nc.sync.dma_start(
+                out=out_1.rearrange("g p m t -> p g (m t)").bitcast(I32)[:, :, ms], in_=y_c[mh][:].bitcast(I32)
+            )
+        for q in range(4):
+            eng = (nc.sync, nc.scalar)[q % 2]
+            eng.dma_start(
+                out=out_2[:, 4 * q : 4 * q + 4, :].rearrange("g r m -> r g m").bitcast(I32),
+                in_=y_sc[32 * q : 32 * q + 4, :, :].bitcast(I32),
+            )

@@ -1,5 +1,4 @@
 from contextlib import ExitStack
-import math
 
 import concourse.mybir as mybir
 
@@ -21,6 +20,7 @@ PARTS = 128
 BANK = 512
 MH = 2
 MW = P // MH
+CHUNKS = ((0, 256), (256, 128), (384, 128))
 
 
 def tile_list_bladder_pressure_reading_kernel(
@@ -44,24 +44,27 @@ def tile_list_bladder_pressure_reading_kernel(
         tab_sc = kt([PARTS, T], U8, "tab_sc")
         w23_sc_raw = kt([PARTS, 2, H], U8, "w23_sc_raw")
         wb_sc_raw = kt([PARTS, 2, 512], U8, "wb_sc_raw")
-        v_sc1 = kt([PARTS, S], U8, "v_sc1")
-        nc.vector.memset(tab_sc[:].bitcast(I32), 0)
+        v_sc = kt([PARTS, 2, S], U8, "v_sc")
+        nc.vector.memset(tab_sc[32:64, :].bitcast(I32), 0)
+        nc.vector.memset(tab_sc[64:128, :].bitcast(I32), 0)
+        nc.vector.memset(v_sc[:].bitcast(I32), 0)
         nc.vector.memset(w23_sc_raw[:].bitcast(I32), 0)
-        nc.vector.memset(v_sc1[:].bitcast(I32), 0)
 
-        tab_w = [kt([PARTS, T], U32, "tab_w%d" % a) for a in range(2)]
-        w1_raw = [kt([PARTS, 4, H], F32, "w1_raw%d" % a) for a in range(2)]
+        w1_raw0 = kt([PARTS, 4, H], F32, "w1_raw0")
         w2_raw = kt([PARTS, 2, H], I32, "w2_raw")
         w3_raw = kt([PARTS, 2, H], U16, "w3_raw")
+        wb_raw = kt([PARTS, 2, 512], U16, "wb_raw")
         gain_t = kt([PARTS, 4], F32, "gain_t")
         vd_t = kt([PARTS, 4], F32, "vd_t")
         w23_sc_in = kt([PARTS, 2, H // 4], I32, "w23_sc_in")
+        tab_w = []
 
-        def load_tab(a):
+        def load_tab(a, tag):
+            tab_w.append(kt([PARTS, T], U32, "tab_w%d" % a, tag))
             nc.sync.dma_start(out=tab_w[a][:].bitcast(I32), in_=tab_words[a].rearrange("p n t -> p (n t)").bitcast(I32))
 
-        def load_w1(a):
-            nc.sync.dma_start(out=w1_raw[a][:], in_=w1[512 * a : 512 * (a + 1), :].rearrange("(p i) c -> p i c", i=4))
+        def load_rows4(dst, src):
+            nc.sync.dma_start(out=dst, in_=src.rearrange("(p i) c -> p i c", i=4))
 
         def load_w_scales(src, row0):
             for q in range(4):
@@ -70,7 +73,6 @@ def tile_list_bladder_pressure_reading_kernel(
                     in_=src[:, 4 * q : 4 * q + 4, :].rearrange("a r c -> r a c").bitcast(I32),
                 )
 
-        wb_raw = kt([PARTS, 2, 512], U16, "wb_raw")
         nc.gpsimd.memset(wb_sc_raw[:].bitcast(I32), 0)
         for q in range(4):
             nc.gpsimd.dma_start(
@@ -78,34 +80,31 @@ def tile_list_bladder_pressure_reading_kernel(
                 in_=wb_scales[0, 4 * q : 4 * q + 4, :].bitcast(I32),
             )
         nc.sync.dma_start(offs_t[:], offs)
-        tab_sc_in = kt([PARTS, T // 4], I32, "tab_sc_in")
-        for q in range(4):
-            nc.sync.dma_start(out=tab_sc_in[32 * q : 32 * q + 8, :], in_=tab_scales[:, 4 * q : 4 * q + 4, :].bitcast(I32))
+        nc.sync.dma_start(out=tab_sc[0:32, :].bitcast(I32), in_=tab_scales.rearrange("a q t -> (a q) t").bitcast(I32))
+        load_w_scales(w2_scales, 4)
         nc.sync.dma_start(out=w3_raw[:].bitcast(I32), in_=w3_words.rearrange("a p c -> p a c").bitcast(I32))
         nc.sync.dma_start(out=w2_raw[:], in_=w2_words.rearrange("a p c i -> p a (c i)").bitcast(I32))
-        load_w1(0)
-        load_w_scales(w2_scales, 4)
-        nc.sync.dma_start(out=wb_raw[:].rearrange("p g c -> p (g c)").bitcast(I32), in_=wb_words[0].bitcast(I32))
-        load_tab(0)
         load_w_scales(w3_scales, 0)
+        load_rows4(w1_raw0[:], w1[0:512, :])
+        nc.sync.dma_start(out=wb_raw[:].rearrange("p g c -> p (g c)").bitcast(I32), in_=wb_words[0].bitcast(I32))
         nc.sync.dma_start(out=gain_t[:], in_=gain.rearrange("(p t) -> p t", t=4))
         nc.sync.dma_start(out=vd_t[:], in_=vd.rearrange("(p t) -> p t", t=4))
-        load_tab(1)
-        load_w1(1)
         nc.sync.dma_start(pos1_t[:], pos1)
         nc.sync.dma_start(pos2_t[:], pos2)
+        load_tab(0, "")
 
-        v_sc = kt([PARTS, S], U8, "v_sc")
-        for q in range(4):
-            rows = slice(32 * q, 32 * q + 8)
-            nc.vector.tensor_copy(tab_sc[rows, :].bitcast(I32), tab_sc_in[rows, :])
-        nc.vector.tensor_copy(v_sc[:], tab_sc[:].indirect(offs_t[:]))
-        for q in range(4):
-            nc.sync.dma_start(
-                out=v_sc1[32 * q : 32 * q + 4, :].bitcast(I32), in_=v_sc[32 * q + 4 : 32 * q + 8, :].bitcast(I32)
-            )
-        ga_t = kt([PARTS, 4, P], F32, "ga_t", "tab_sc")
-        nc.sync.dma_start(out=ga_t[:], in_=ga.rearrange("(p t) m -> p t m", t=4))
+        v_sc_rows = kt([PARTS, S], U8, "v_sc_rows")
+        nc.vector.tensor_copy(v_sc_rows[:], tab_sc[:].indirect(offs_t[:]))
+        nc.vector.tensor_copy(v_sc[0:4, 0, :].bitcast(I32), v_sc_rows[0:4, :].bitcast(I32))
+
+        def place_scale_rows(a, q):
+            row = 16 * a + 4 * q
+            nc.sync.dma_start(out=v_sc[32 * q : 32 * q + 4, a, :].bitcast(I32), in_=v_sc_rows[row : row + 4, :].bitcast(I32))
+
+        for a, q in ((0, 1), (0, 2), (0, 3), (1, 0), (1, 1), (1, 2)):
+            place_scale_rows(a, q)
+        load_tab(1, "tab_sc")
+        place_scale_rows(1, 3)
         v_w = [[kt([PARTS, BANK], U32, "v_w%d_%d" % (a, jh)) for jh in range(2)] for a in range(2)]
 
         def gather_tab(a):
@@ -114,13 +113,13 @@ def tile_list_bladder_pressure_reading_kernel(
 
         def deal(dst, src):
             nc.vector.tensor_copy(
-                out=dst.rearrange("p a (t m) -> p a m t", t=4), in_=src.rearrange("p a (m t) -> p a m t", t=4)
+                out=dst.rearrange("p a (t m) -> p a t m", t=4), in_=src.rearrange("p a (m t) -> p a t m", t=4)
             )
 
-        def round_weight(eng, raw, name, tag):
-            wbf = kt([PARTS, 4, PARTS, 4], BF16, name, tag)
+        def round_weight(eng, raw, name, tag, t0=0, t1=4):
+            wbf = kt([PARTS, t1 - t0, PARTS, 4], BF16, name, tag)
             o = wbf[:].rearrange("p t m i -> p m i t")
-            s = raw[:].rearrange("p i (m t) -> p m i t", t=4)
+            s = raw[:].rearrange("p i (m t) -> p m i t", t=4)[:, :, :, t0:t1]
             if eng == "scalar":
                 nc.scalar.copy(out=o, in_=s)
             else:
@@ -134,90 +133,100 @@ def tile_list_bladder_pressure_reading_kernel(
         w3_c = kt([PARTS, 2, H], U16, "w3_c")
         w23_sc = kt([PARTS, 2, H], U8, "w23_sc")
         deal(w2_c[:].bitcast(I32), w2_raw[:])
+        late = kt([PARTS, 4 * 4 * 512], F32, "late", "w2_raw")
+        w1_raw1, ga_t, wa0_raw, wa1_raw = (
+            late[:, 2048 * u : 2048 * (u + 1)].rearrange("p (i c) -> p i c", i=4) for u in range(4)
+        )
+        wa_raw = [wa0_raw, wa1_raw]
+        load_rows4(w1_raw1, w1[512:1024, :])
+        load_rows4(ga_t, ga)
+        for g in range(2):
+            load_rows4(wa_raw[g], wa[:, 512 * g : 512 * (g + 1)])
         deal(w3_c[:], w3_raw[:])
         wb_c = kt([PARTS, 2, 512], U16, "wb_c")
         deal(wb_c[:], wb_raw[:])
-        w1_c = [kt([PARTS, H], U32, "w1_c%d" % a) for a in range(2)]
-        w1_sc = [kt([PARTS, H], U8, "w1_sc%d" % a) for a in range(2)]
-        wbf = round_weight("scalar", w1_raw[0], "w1bf0", "")
-        quantize(w1_c[0][:], w1_sc[0][:], wbf[:].rearrange("p t m i -> p (t m i)"))
-        gather_tab(0)
         for q in range(4):
             rows = slice(32 * q, 32 * q + 8)
             nc.vector.tensor_copy(w23_sc_raw[rows, :, :].bitcast(I32), w23_sc_in[rows, :, :])
         deal(w23_sc[:], w23_sc_raw[:])
+        w1_c = [kt([PARTS, H], U32, "w1_c%d" % a) for a in range(2)]
+        w1_sc = [kt([PARTS, H], U8, "w1_sc%d" % a) for a in range(2)]
+        wbf = round_weight("scalar", w1_raw0, "w1bf0", "")
+        quantize(w1_c[0][:], w1_sc[0][:], wbf[:].rearrange("p t m i -> p (t m i)"))
+        gather_tab(0)
         gather_tab(1)
-        wbf = round_weight("vector", w1_raw[1], "w1bf1", "tab_w1")
-        quantize(w1_c[1][:], w1_sc[1][:], wbf[:].rearrange("p t m i -> p (t m i)"))
+        wbf = round_weight("vector", w1_raw1, "w1bf1", "tab_sc", 0, 2)
+        quantize(w1_c[1][:, :256], w1_sc[1][:, :256], wbf[:].rearrange("p t m i -> p (t m i)"))
 
-        wa_both = kt([PARTS, 2, 4, 512], F32, "wa_both", "tab_w0")
-        wa_raw = [wa_both[:, g] for g in range(2)]
-        for g in range(2):
-            nc.sync.dma_start(out=wa_raw[g][:], in_=wa[:, 512 * g : 512 * (g + 1)].rearrange("(p i) c -> p i c", i=4))
         res_v = res.rearrange("(g p t) m -> g p t m", g=2, t=4)
-        y = []
+        y = {}
 
-        def load_res(mh, tag):
-            y.append(kt([PARTS, 2, 4, MW], F32, "y%d" % mh, tag))
-            for g in range(2):
-                nc.sync.dma_start(out=y[mh][:, g], in_=res_v[g, :, :, MW * mh : MW * (mh + 1)])
+        def load_res(chunks, tag):
+            width = sum(w for m0, w in chunks)
+            buf = kt([PARTS, 8 * width], F32, "y%d" % chunks[0][0], tag)
+            at = 0
+            for m0, w in chunks:
+                for g in range(2):
+                    y[m0, g] = buf[:, at : at + 4 * w].rearrange("p (t m) -> p t m", t=4)
+                    nc.sync.dma_start(out=y[m0, g], in_=res_v[g, :, :, m0 : m0 + w])
+                    at = at + 4 * w
 
-        load_res(0, "tab_w1")
+        load_res(CHUNKS[:1], "tab_sc")
 
         gv = kt([PARTS, 4], F32, "gv")
         nc.gpsimd.tensor_tensor(gv[:], gain_t[:], vd_t[:], ALU.mult)
         gv_wide = kt([PARTS, 4, MW], F32, "gv_wide", "w1_raw0")
         nc.scalar.copy(out=gv_wide[:], in_=gv[:].unsqueeze(2).to_broadcast([PARTS, 4, MW]))
-        gag = kt([PARTS, 4, P], F32, "gag", "w1_raw1")
-        for t in range(4):
-            nc.gpsimd.tensor_scalar(gag[:, t, :], ga_t[:, t, :], gain_t[:, t : t + 1], 0.0, ALU.mult, ALU.add)
 
         h = [kt([PARTS, S], F32, "h%d" % t) for t in range(4)]
         wa_c = [kt([PARTS, 512], U32, "wa_c%d" % g) for g in range(2)]
         wa_sc = [kt([PARTS, 512], U8, "wa_sc%d" % g) for g in range(2)]
 
-        def products(t, jh):
+        def product(tag, bufs, t, jh, codes, dt, scales):
             cols = slice(PARTS * t, PARTS * (t + 1))
             js = slice(BANK * jh, BANK * (jh + 1))
-            pb = psum.tile([PARTS, BANK], F32, name="pb", tag="pb", bufs=2)
-            pa = psum.tile([PARTS, BANK], F32, name="pa", tag="pa", bufs=3)
-            pd = psum.tile([PARTS, BANK], F32, name="pd", tag="pd", bufs=3)
+            acc = psum.tile([PARTS, BANK], F32, name=tag, tag=tag, bufs=bufs)
             for a in range(2):
                 nc.tensor.matmul_mx(
-                    out=pb[:], lhsT=w2_c[:, a, cols].bitcast(FP8X4), lhsT_scale=w23_sc[4:, a, cols],
-                    rhs=v_w[a][jh][:].bitcast(FP8X4), rhs_scale=v_sc[4 * a :, js], start=a == 0, stop=a == 1,
+                    out=acc[:], lhsT=codes[a][:, cols].bitcast(dt), lhsT_scale=scales[a][:, cols],
+                    rhs=v_w[a][jh][:].bitcast(FP8X4), rhs_scale=v_sc[:, a, js], start=a == 0, stop=a == 1,
                 )
-            for a in range(2):
-                nc.tensor.matmul_mx(
-                    out=pa[:], lhsT=w1_c[a][:, cols].bitcast(FP8X4), lhsT_scale=w1_sc[a][:, cols],
-                    rhs=v_w[a][jh][:].bitcast(FP8X4), rhs_scale=v_sc[4 * a :, js], start=a == 0, stop=a == 1,
-                )
-            for a in range(2):
-                nc.tensor.matmul_mx(
-                    out=pd[:], lhsT=w3_c[:, a, cols].bitcast(FP4X4), lhsT_scale=w23_sc[:, a, cols],
-                    rhs=v_w[a][jh][:].bitcast(FP8X4), rhs_scale=(v_sc, v_sc1)[a][:, js], start=a == 0, stop=a == 1,
-                )
-            mag = ring.tile([PARTS, BANK], F32, name="mag")
-            cosb = kt([PARTS, BANK], F32, "cos%d_%d" % (t, jh))
-            nc.scalar.activation(mag[:], pb[:], ACT.Abs)
-            nc.scalar.activation(cosb[:], mag[:], ACT.Sin, bias=math.pi / 2, scale=-1.0)
-            return pa, pd, cosb
+            return acc
 
-        def slice_of_h(t):
-            parts = [products(t, jh) for jh in range(2)]
+        cosb = {}
+        gag = []
+
+        def cosine(t, jh):
+            pb = product("pb", 2, t, jh, [w2_c[:, a] for a in range(2)], FP8X4, [w23_sc[4:, a] for a in range(2)])
+            mag = kt([PARTS, BANK], F32, "mag", "mag_first" if (t, jh) == (0, 1) else "mag%d" % jh)
+            cosb[t, jh] = kt([PARTS, BANK], F32, "cos%d_%d" % (t, jh))
+            nc.scalar.activation(mag[:], pb[:], ACT.Sin, scale=0.5)
+            nc.scalar.activation(cosb[t, jh][:], mag[:], ACT.Square)
+
+        def linear_parts(t):
+            pa = [product("pa", 3, t, jh, w1_c, FP8X4, w1_sc) for jh in range(2)]
+            pd = [
+                product("pd", 3, t, jh, [w3_c[:, a] for a in range(2)], FP4X4, [w23_sc[:, a] for a in range(2)])
+                for jh in range(2)
+            ]
+            return pa, pd
+
+        def slice_of_h(t, pa, pd):
             prods = []
-            for pa, pd, cosb in parts:
+            for jh in range(2):
                 prod = ring.tile([PARTS, BANK], F32, name="prod")
-                nc.vector.tensor_tensor(prod[:], pa[:], cosb[:], ALU.mult)
+                nc.vector.scalar_tensor_tensor(prod[:], cosb[t, jh][:], 0.5, pa[jh][:], ALU.subtract, ALU.mult)
                 prods.append(prod)
             for jh in range(2):
-                nc.vector.tensor_tensor(h[t][:, BANK * jh : BANK * (jh + 1)], parts[jh][1][:], prods[jh][:], ALU.max)
+                nc.vector.scalar_tensor_tensor(
+                    h[t][:, BANK * jh : BANK * (jh + 1)], prods[jh][:], -2.0, pd[jh][:], ALU.mult, ALU.max
+                )
 
         def pick(t, mh, xa_g, xb_g):
             ms = slice(MW * mh, MW * (mh + 1))
             lo, hi = ms.start // 16, ms.stop // 16
             nc.vector.tensor_tensor(xa_g[:, t, :], h[t][:].indirect(pos1_t[:, lo:hi]), gv_wide[:, t, :], ALU.mult)
-            nc.vector.tensor_tensor(xb_g[:, t, :], h[t][:].indirect(pos2_t[:, lo:hi]), gag[:, t, ms], ALU.mult)
+            nc.vector.tensor_tensor(xb_g[:, t, :], h[t][:].indirect(pos2_t[:, lo:hi]), gag[t][:, ms], ALU.mult)
 
         def interleave(dst, src):
             nc.scalar.copy(
@@ -226,66 +235,81 @@ def tile_list_bladder_pressure_reading_kernel(
 
         x_c, x_sc = {}, {}
 
-        def finish_x(mh, xa_g, xb_g):
-            for nm, src in (("a", xa_g), ("b", xb_g)):
-                xbf = kt([PARTS, MW, 4], BF16, "xbf%s%d" % (nm, mh))
-                interleave(xbf[:], src[:])
-                x_c[nm, mh] = kt([PARTS, MW], U32, "x_c%s%d" % (nm, mh))
-                x_sc[nm, mh] = kt([PARTS, MW], U8, "x_sc%s%d" % (nm, mh))
-                quantize(x_c[nm, mh][:], x_sc[nm, mh][:], xbf[:].rearrange("p m t -> p (m t)"))
+        def finish_x(mh, nm, src, xbf):
+            interleave(xbf.rearrange("p (m t) -> p m t", t=4), src)
+            x_c[nm, mh] = kt([PARTS, MW], U32, "x_c%s%d" % (nm, mh))
+            x_sc[nm, mh] = kt([PARTS, MW], U8, "x_sc%s%d" % (nm, mh))
+            quantize(x_c[nm, mh][:], x_sc[nm, mh][:], xbf)
 
-        xa_g = kt([PARTS, 4, MW], F32, "xa_g0")
-        xb_g = kt([PARTS, 4, MW], F32, "xb_g0")
+        def rows4(tile):
+            return tile[:].rearrange("p (t m) -> p t m", t=4)
+
+        xa_g = rows4(kt([PARTS, 4 * MW], F32, "xa_g0"))
+        xb_g = rows4(kt([PARTS, 4 * MW], F32, "xb_g0"))
+        for jh in range(2):
+            cosine(0, jh)
+        w1_rest = round_weight("scalar", w1_raw1, "w1bf2", "mag_first", 2, 4)
         for t in range(4):
-            slice_of_h(t)
+            pa, pd = linear_parts(t)
+            if t < 3:
+                for jh in range(2):
+                    cosine(t + 1, jh)
+            slice_of_h(t, pa, pd)
+            if t == 0:
+                quantize(w1_c[1][:, 256:], w1_sc[1][:, 256:], w1_rest[:].rearrange("p t m i -> p (t m i)"))
+            gag.append(kt([PARTS, P], F32, "gag%d" % t, "cos%d_1" % (t - 1) if t else "mag_first"))
+            nc.scalar.activation(gag[t][:], ga_t[:, t, :], ACT.Copy, scale=gain_t[:, t : t + 1])
             pick(t, 0, xa_g, xb_g)
             if t == 0:
-                load_res(1, "cos0_0")
+                load_res(CHUNKS[1:], "cos0_0")
             if t == 1:
                 wb_sc = kt([PARTS, 2, 512], U8, "wb_sc", "cos1_0")
                 deal(wb_sc[:], wb_sc_raw[:])
-            if t in (1, 2):
-                g = t - 1
-                wbf = round_weight("scalar", wa_raw[g], "wabf%d" % g, "cos%d_1" % t)
+            if t in (2, 3):
+                g = t - 2
+                wbf = round_weight("scalar", wa_raw[g], "wabf%d" % g, "mag%d" % g)
                 quantize(wa_c[g][:], wa_sc[g][:], wbf[:].rearrange("p t m i -> p (t m i)"))
-        finish_x(0, xa_g, xb_g)
-        xa_g = kt([PARTS, 4, MW], F32, "xa_g1", "cos3_0")
-        xb_g = kt([PARTS, 4, MW], F32, "xb_g1", "cos3_1")
+        xa_late = kt([PARTS, 4 * MW], F32, "xa_g1", "cos3_0")
+        xb_late = kt([PARTS, 4 * MW], F32, "xb_g1", "cos3_1")
+        finish_x(0, "a", xa_g, xa_late[:, 2 * MW :].bitcast(BF16))
+        finish_x(0, "b", xb_g, xb_late[:, 2 * MW :].bitcast(BF16))
         for t in range(4):
-            pick(t, 1, xa_g, xb_g)
-        finish_x(1, xa_g, xb_g)
+            pick(t, 1, rows4(xa_late), rows4(xb_late))
+        finish_x(1, "a", rows4(xa_late), kt([PARTS, 4 * MW], BF16, "xbfa1")[:])
+        finish_x(1, "b", rows4(xb_late), kt([PARTS, 4 * MW], BF16, "xbfb1")[:])
 
-        y_c = [kt([PARTS, 2, MW], U32, "y_c%d" % mh) for mh in range(MH)]
         y_sc = kt([PARTS, 2, P], U8, "y_sc")
         out_y = out_0.rearrange("(g p t) m -> g p t m", g=2, t=4)
-        per_bank = BANK // MW
+        out_words = out_1.rearrange("g p m t -> p g (m t)").bitcast(I32)
         n_bank = 0
-        for mh in range(MH):
-            ms = slice(MW * mh, MW * (mh + 1))
+        for m0, w in CHUNKS:
+            mh = m0 // MW
+            ms = slice(m0, m0 + w)
+            xs = slice(m0 - MW * mh, m0 - MW * mh + w)
+            per_bank = BANK // w
+            y_c = kt([PARTS, 2, w], U32, "y_c%d" % m0)
             for g in range(2):
                 for t0 in range(0, 4, per_bank):
                     tag, bufs = (("pb", 2), ("pa", 3), ("pd", 3))[n_bank % 3]
                     n_bank = n_bank + 1
-                    py = psum.tile([PARTS, per_bank, MW], F32, name="py", tag=tag, bufs=bufs)
+                    py = psum.tile([PARTS, per_bank, w], F32, name="py", tag=tag, bufs=bufs)
                     for u in range(per_bank):
                         cols = slice(PARTS * (t0 + u), PARTS * (t0 + u + 1))
                         nc.tensor.matmul_mx(
-                            out=py[:, u, :], lhsT=wb_c[:, g, cols].bitcast(FP4X4), lhsT_scale=wb_sc[:, g, cols],
-                            rhs=x_c["b", mh][:].bitcast(FP8X4), rhs_scale=x_sc["b", mh][:], start=True, stop=False,
+                            out=py[:, u, :], lhsT=wa_c[g][:, cols].bitcast(FP8X4), lhsT_scale=wa_sc[g][:, cols],
+                            rhs=x_c["a", mh][:, xs].bitcast(FP8X4), rhs_scale=x_sc["a", mh][:, xs], start=True, stop=False,
                         )
                         nc.tensor.matmul_mx(
-                            out=py[:, u, :], lhsT=wa_c[g][:, cols].bitcast(FP8X4), lhsT_scale=wa_sc[g][:, cols],
-                            rhs=x_c["a", mh][:].bitcast(FP8X4), rhs_scale=x_sc["a", mh][:], start=False, stop=True,
+                            out=py[:, u, :], lhsT=wb_c[:, g, cols].bitcast(FP4X4), lhsT_scale=wb_sc[:, g, cols],
+                            rhs=x_c["b", mh][:, xs].bitcast(FP8X4), rhs_scale=x_sc["b", mh][:, xs], start=False, stop=True,
                         )
                     ts = slice(t0, t0 + per_bank)
-                    nc.vector.tensor_tensor(y[mh][:, g, ts, :], py[:], y[mh][:, g, ts, :], ALU.add)
-                nc.sync.dma_start(out=out_y[g, :, :, ms], in_=y[mh][:, g])
-                ybf = ring.tile([PARTS, MW, 4], BF16, name="ybf", align_bytes=64)
-                interleave(ybf[:], y[mh][:, g])
-                quantize(y_c[mh][:, g, :], y_sc[:, g, ms], ybf[:].rearrange("p m t -> p (m t)"))
-            nc.sync.dma_start(
-                out=out_1.rearrange("g p m t -> p g (m t)").bitcast(I32)[:, :, ms], in_=y_c[mh][:].bitcast(I32)
-            )
+                    nc.vector.tensor_tensor(y[m0, g][:, ts, :], py[:], y[m0, g][:, ts, :], ALU.add)
+                nc.sync.dma_start(out=out_y[g, :, :, ms], in_=y[m0, g])
+                ybf = kt([PARTS, w, 4], BF16, "ybf%d_%d" % (m0, g))
+                interleave(ybf[:], y[m0, g])
+                quantize(y_c[:, g, :], y_sc[:, g, ms], ybf[:].rearrange("p m t -> p (m t)"))
+            nc.sync.dma_start(out=out_words[:, :, ms], in_=y_c[:].bitcast(I32))
         for q in range(4):
             eng = (nc.sync, nc.scalar)[q % 2]
             eng.dma_start(

from contextlib import ExitStack

import concourse.mybir as mybir

K, H, N, T, S, P = 1024, 512, 1024, 4096, 1024, 512
FLOPS = 2 * (3 * K * H * S + 2 * H * N * P)

F32 = mybir.dt.float32
BF16 = mybir.dt.bfloat16
I32 = mybir.dt.int32
U32 = mybir.dt.uint32
U16 = mybir.dt.uint16
U8 = mybir.dt.uint8
FP8X4 = mybir.dt.float8_e4m3fn_x4
FP4X4 = mybir.dt.float4_e2m1fn_x4
ALU = mybir.AluOpType
ACT = mybir.ActivationFunctionType

PARTS = 128
BANK = 512
MH = 2
MW = P // MH
CHUNKS = ((0, 256), (256, 128), (384, 128))


def tile_list_bladder_pressure_reading_kernel(
    tc, tab_words, tab_scales, offs, w1, w2_words, w2_scales, w3_words, w3_scales, gain, pos1, pos2, vd, ga, wa,
    wb_words, wb_scales, res, out_0, out_1, out_2,
):
    nc = tc.nc
    with ExitStack() as ctx:
        lists = ctx.enter_context(tc.tile_pool(name="lists", bufs=1))
        keep = ctx.enter_context(tc.tile_pool(name="keep", bufs=1))
        ring = ctx.enter_context(tc.tile_pool(name="ring", bufs=2))
        psum = ctx.enter_context(tc.psum_pool(name="psum", bufs=1))

        def kt(shape, dt, name, tag=""):
            return keep.tile(shape, dt, name=name, tag=tag or name, align_bytes=64)

        offs_t = lists.tile([PARTS, S // 16], U16, name="offs_t")
        pos1_t = lists.tile([PARTS, P // 16], U16, name="pos1_t")
        pos2_t = lists.tile([PARTS, P // 16], U16, name="pos2_t")

        tab_sc = kt([PARTS, T], U8, "tab_sc")
        w23_sc_raw = kt([PARTS, 2, H], U8, "w23_sc_raw")
        wb_sc_raw = kt([PARTS, 2, 512], U8, "wb_sc_raw")
        v_sc = kt([PARTS, 2, S], U8, "v_sc")
        nc.vector.memset(tab_sc[32:64, :].bitcast(I32), 0)
        nc.vector.memset(tab_sc[64:128, :].bitcast(I32), 0)
        nc.vector.memset(v_sc[:].bitcast(I32), 0)
        nc.vector.memset(w23_sc_raw[:].bitcast(I32), 0)

        w1_raw0 = kt([PARTS, 4, H], F32, "w1_raw0")
        w2_raw = kt([PARTS, 2, H], I32, "w2_raw")
        w3_raw = kt([PARTS, 2, H], U16, "w3_raw")
        wb_raw = kt([PARTS, 2, 512], U16, "wb_raw")
        gain_t = kt([PARTS, 4], F32, "gain_t")
        vd_t = kt([PARTS, 4], F32, "vd_t")
        w23_sc_in = kt([PARTS, 2, H // 4], I32, "w23_sc_in")
        tab_w = []

        def load_tab(a, tag):
            tab_w.append(kt([PARTS, T], U32, "tab_w%d" % a, tag))
            nc.sync.dma_start(out=tab_w[a][:].bitcast(I32), in_=tab_words[a].rearrange("p n t -> p (n t)").bitcast(I32))

        def load_rows4(dst, src):
            nc.sync.dma_start(out=dst, in_=src.rearrange("(p i) c -> p i c", i=4))

        def load_w_scales(src, row0):
            for q in range(4):
                nc.sync.dma_start(
                    out=w23_sc_in[32 * q + row0 : 32 * q + row0 + 4, :, :],
                    in_=src[:, 4 * q : 4 * q + 4, :].rearrange("a r c -> r a c").bitcast(I32),
                )

        nc.gpsimd.memset(wb_sc_raw[:].bitcast(I32), 0)
        for q in range(4):
            nc.gpsimd.dma_start(
                out=wb_sc_raw[32 * q : 32 * q + 4, :, :].rearrange("p g c -> p (g c)").bitcast(I32),
                in_=wb_scales[0, 4 * q : 4 * q + 4, :].bitcast(I32),
            )
        nc.sync.dma_start(offs_t[:], offs)
        nc.sync.dma_start(out=tab_sc[0:32, :].bitcast(I32), in_=tab_scales.rearrange("a q t -> (a q) t").bitcast(I32))
        load_w_scales(w2_scales, 4)
        nc.sync.dma_start(out=w3_raw[:].bitcast(I32), in_=w3_words.rearrange("a p c -> p a c").bitcast(I32))
        nc.sync.dma_start(out=w2_raw[:], in_=w2_words.rearrange("a p c i -> p a (c i)").bitcast(I32))
        load_w_scales(w3_scales, 0)
        load_rows4(w1_raw0[:], w1[0:512, :])
        nc.sync.dma_start(out=wb_raw[:].rearrange("p g c -> p (g c)").bitcast(I32), in_=wb_words[0].bitcast(I32))
        nc.sync.dma_start(out=gain_t[:], in_=gain.rearrange("(p t) -> p t", t=4))
        nc.sync.dma_start(out=vd_t[:], in_=vd.rearrange("(p t) -> p t", t=4))
        nc.sync.dma_start(pos1_t[:], pos1)
        nc.sync.dma_start(pos2_t[:], pos2)
        load_tab(0, "")

        v_sc_rows = kt([PARTS, S], U8, "v_sc_rows")
        nc.vector.tensor_copy(v_sc_rows[:], tab_sc[:].indirect(offs_t[:]))
        nc.vector.tensor_copy(v_sc[0:4, 0, :].bitcast(I32), v_sc_rows[0:4, :].bitcast(I32))

        def place_scale_rows(a, q):
            row = 16 * a + 4 * q
            nc.sync.dma_start(out=v_sc[32 * q : 32 * q + 4, a, :].bitcast(I32), in_=v_sc_rows[row : row + 4, :].bitcast(I32))

        for a, q in ((0, 1), (0, 2), (0, 3), (1, 0), (1, 1), (1, 2)):
            place_scale_rows(a, q)
        load_tab(1, "tab_sc")
        place_scale_rows(1, 3)
        v_w = [[kt([PARTS, BANK], U32, "v_w%d_%d" % (a, jh)) for jh in range(2)] for a in range(2)]

        def gather_tab(a):
            for jh in range(2):
                nc.vector.tensor_copy(v_w[a][jh][:], tab_w[a][:].indirect(offs_t[:, 32 * jh : 32 * (jh + 1)]))

        def deal(dst, src):
            nc.vector.tensor_copy(
                out=dst.rearrange("p a (t m) -> p a t m", t=4), in_=src.rearrange("p a (m t) -> p a t m", t=4)
            )

        def round_weight(eng, raw, name, tag, t0=0, t1=4):
            wbf = kt([PARTS, t1 - t0, PARTS, 4], BF16, name, tag)
            o = wbf[:].rearrange("p t m i -> p m i t")
            s = raw[:].rearrange("p i (m t) -> p m i t", t=4)[:, :, :, t0:t1]
            if eng == "scalar":
                nc.scalar.copy(out=o, in_=s)
            else:
                nc.vector.tensor_copy(out=o, in_=s)
            return wbf

        def quantize(codes, scales, src):
            nc.vector.quantize_mx(out=codes.bitcast(FP8X4), scales=scales, in_=src)

        w2_c = kt([PARTS, 2, H], U32, "w2_c")
        w3_c = kt([PARTS, 2, H], U16, "w3_c")
        w23_sc = kt([PARTS, 2, H], U8, "w23_sc")
        deal(w2_c[:].bitcast(I32), w2_raw[:])
        late = kt([PARTS, 4 * 4 * 512], F32, "late", "w2_raw")
        w1_raw1, ga_t, wa0_raw, wa1_raw = (
            late[:, 2048 * u : 2048 * (u + 1)].rearrange("p (i c) -> p i c", i=4) for u in range(4)
        )
        wa_raw = [wa0_raw, wa1_raw]
        load_rows4(w1_raw1, w1[512:1024, :])
        load_rows4(ga_t, ga)
        for g in range(2):
            load_rows4(wa_raw[g], wa[:, 512 * g : 512 * (g + 1)])
        deal(w3_c[:], w3_raw[:])
        wb_c = kt([PARTS, 2, 512], U16, "wb_c")
        deal(wb_c[:], wb_raw[:])
        for q in range(4):
            rows = slice(32 * q, 32 * q + 8)
            nc.vector.tensor_copy(w23_sc_raw[rows, :, :].bitcast(I32), w23_sc_in[rows, :, :])
        deal(w23_sc[:], w23_sc_raw[:])
        w1_c = [kt([PARTS, H], U32, "w1_c%d" % a) for a in range(2)]
        w1_sc = [kt([PARTS, H], U8, "w1_sc%d" % a) for a in range(2)]
        wbf = round_weight("scalar", w1_raw0, "w1bf0", "")
        quantize(w1_c[0][:], w1_sc[0][:], wbf[:].rearrange("p t m i -> p (t m i)"))
        gather_tab(0)
        gather_tab(1)
        wbf = round_weight("vector", w1_raw1, "w1bf1", "tab_sc", 0, 2)
        quantize(w1_c[1][:, :256], w1_sc[1][:, :256], wbf[:].rearrange("p t m i -> p (t m i)"))

        res_v = res.rearrange("(g p t) m -> g p t m", g=2, t=4)
        y = {}

        def load_res(chunks, tag):
            width = sum(w for m0, w in chunks)
            buf = kt([PARTS, 8 * width], F32, "y%d" % chunks[0][0], tag)
            at = 0
            for m0, w in chunks:
                for g in range(2):
                    y[m0, g] = buf[:, at : at + 4 * w].rearrange("p (t m) -> p t m", t=4)
                    nc.sync.dma_start(out=y[m0, g], in_=res_v[g, :, :, m0 : m0 + w])
                    at = at + 4 * w

        load_res(CHUNKS[:1], "tab_sc")

        gv = kt([PARTS, 4], F32, "gv")
        nc.gpsimd.tensor_tensor(gv[:], gain_t[:], vd_t[:], ALU.mult)
        gv_wide = kt([PARTS, 4, MW], F32, "gv_wide", "w1_raw0")
        nc.scalar.copy(out=gv_wide[:], in_=gv[:].unsqueeze(2).to_broadcast([PARTS, 4, MW]))

        h = [kt([PARTS, S], F32, "h%d" % t) for t in range(4)]
        wa_c = [kt([PARTS, 512], U32, "wa_c%d" % g) for g in range(2)]
        wa_sc = [kt([PARTS, 512], U8, "wa_sc%d" % g) for g in range(2)]

        def product(tag, bufs, t, jh, codes, dt, scales):
            cols = slice(PARTS * t, PARTS * (t + 1))
            js = slice(BANK * jh, BANK * (jh + 1))
            acc = psum.tile([PARTS, BANK], F32, name=tag, tag=tag, bufs=bufs)
            for a in range(2):
                nc.tensor.matmul_mx(
                    out=acc[:], lhsT=codes[a][:, cols].bitcast(dt), lhsT_scale=scales[a][:, cols],
                    rhs=v_w[a][jh][:].bitcast(FP8X4), rhs_scale=v_sc[:, a, js], start=a == 0, stop=a == 1,
                )
            return acc

        cosb = {}
        gag = []

        def cosine(t, jh):
            pb = product("pb", 2, t, jh, [w2_c[:, a] for a in range(2)], FP8X4, [w23_sc[4:, a] for a in range(2)])
            mag = kt([PARTS, BANK], F32, "mag", "mag_first" if (t, jh) == (0, 1) else "mag%d" % jh)
            cosb[t, jh] = kt([PARTS, BANK], F32, "cos%d_%d" % (t, jh))
            nc.scalar.activation(mag[:], pb[:], ACT.Sin, scale=0.5)
            nc.scalar.activation(cosb[t, jh][:], mag[:], ACT.Square)

        def linear_parts(t):
            pa = [product("pa", 3, t, jh, w1_c, FP8X4, w1_sc) for jh in range(2)]
            pd = [
                product("pd", 3, t, jh, [w3_c[:, a] for a in range(2)], FP4X4, [w23_sc[:, a] for a in range(2)])
                for jh in range(2)
            ]
            return pa, pd

        def slice_of_h(t, pa, pd):
            prods = []
            for jh in range(2):
                prod = ring.tile([PARTS, BANK], F32, name="prod")
                nc.vector.scalar_tensor_tensor(prod[:], cosb[t, jh][:], 0.5, pa[jh][:], ALU.subtract, ALU.mult)
                prods.append(prod)
            for jh in range(2):
                nc.vector.scalar_tensor_tensor(
                    h[t][:, BANK * jh : BANK * (jh + 1)], prods[jh][:], -2.0, pd[jh][:], ALU.mult, ALU.max
                )

        def pick(t, mh, xa_g, xb_g):
            ms = slice(MW * mh, MW * (mh + 1))
            lo, hi = ms.start // 16, ms.stop // 16
            nc.vector.tensor_tensor(xa_g[:, t, :], h[t][:].indirect(pos1_t[:, lo:hi]), gv_wide[:, t, :], ALU.mult)
            nc.vector.tensor_tensor(xb_g[:, t, :], h[t][:].indirect(pos2_t[:, lo:hi]), gag[t][:, ms], ALU.mult)

        def interleave(dst, src):
            nc.scalar.copy(
                out=dst.rearrange("p (c i) t -> p c t i", i=4), in_=src.rearrange("p t (c i) -> p c t i", i=4)
            )

        x_c, x_sc = {}, {}

        def finish_x(mh, nm, src, xbf):
            interleave(xbf.rearrange("p (m t) -> p m t", t=4), src)
            x_c[nm, mh] = kt([PARTS, MW], U32, "x_c%s%d" % (nm, mh))
            x_sc[nm, mh] = kt([PARTS, MW], U8, "x_sc%s%d" % (nm, mh))
            quantize(x_c[nm, mh][:], x_sc[nm, mh][:], xbf)

        def rows4(tile):
            return tile[:].rearrange("p (t m) -> p t m", t=4)

        xa_g = rows4(kt([PARTS, 4 * MW], F32, "xa_g0"))
        xb_g = rows4(kt([PARTS, 4 * MW], F32, "xb_g0"))
        for jh in range(2):
            cosine(0, jh)
        w1_rest = round_weight("scalar", w1_raw1, "w1bf2", "mag_first", 2, 4)
        for t in range(4):
            pa, pd = linear_parts(t)
            if t < 3:
                for jh in range(2):
                    cosine(t + 1, jh)
            slice_of_h(t, pa, pd)
            if t == 0:
                quantize(w1_c[1][:, 256:], w1_sc[1][:, 256:], w1_rest[:].rearrange("p t m i -> p (t m i)"))
            gag.append(kt([PARTS, P], F32, "gag%d" % t, "cos%d_1" % (t - 1) if t else "mag_first"))
            nc.scalar.activation(gag[t][:], ga_t[:, t, :], ACT.Copy, scale=gain_t[:, t : t + 1])
            pick(t, 0, xa_g, xb_g)
            if t == 0:
                load_res(CHUNKS[1:], "cos0_0")
            if t == 1:
                wb_sc = kt([PARTS, 2, 512], U8, "wb_sc", "cos1_0")
                deal(wb_sc[:], wb_sc_raw[:])
            if t in (2, 3):
                g = t - 2
                wbf = round_weight("scalar", wa_raw[g], "wabf%d" % g, "mag%d" % g)
                quantize(wa_c[g][:], wa_sc[g][:], wbf[:].rearrange("p t m i -> p (t m i)"))
        xa_late = kt([PARTS, 4 * MW], F32, "xa_g1", "cos3_0")
        xb_late = kt([PARTS, 4 * MW], F32, "xb_g1", "cos3_1")
        finish_x(0, "a", xa_g, xa_late[:, 2 * MW :].bitcast(BF16))
        finish_x(0, "b", xb_g, xb_late[:, 2 * MW :].bitcast(BF16))
        for t in range(4):
            pick(t, 1, rows4(xa_late), rows4(xb_late))
        finish_x(1, "a", rows4(xa_late), kt([PARTS, 4 * MW], BF16, "xbfa1")[:])
        finish_x(1, "b", rows4(xb_late), kt([PARTS, 4 * MW], BF16, "xbfb1")[:])

        y_sc = kt([PARTS, 2, P], U8, "y_sc")
        out_y = out_0.rearrange("(g p t) m -> g p t m", g=2, t=4)
        out_words = out_1.rearrange("g p m t -> p g (m t)").bitcast(I32)
        n_bank = 0
        for m0, w in CHUNKS:
            mh = m0 // MW
            ms = slice(m0, m0 + w)
            xs = slice(m0 - MW * mh, m0 - MW * mh + w)
            per_bank = BANK // w
            y_c = kt([PARTS, 2, w], U32, "y_c%d" % m0)
            for g in range(2):
                for t0 in range(0, 4, per_bank):
                    tag, bufs = (("pb", 2), ("pa", 3), ("pd", 3))[n_bank % 3]
                    n_bank = n_bank + 1
                    py = psum.tile([PARTS, per_bank, w], F32, name="py", tag=tag, bufs=bufs)
                    for u in range(per_bank):
                        cols = slice(PARTS * (t0 + u), PARTS * (t0 + u + 1))
                        nc.tensor.matmul_mx(
                            out=py[:, u, :], lhsT=wa_c[g][:, cols].bitcast(FP8X4), lhsT_scale=wa_sc[g][:, cols],
                            rhs=x_c["a", mh][:, xs].bitcast(FP8X4), rhs_scale=x_sc["a", mh][:, xs], start=True, stop=False,
                        )
                        nc.tensor.matmul_mx(
                            out=py[:, u, :], lhsT=wb_c[:, g, cols].bitcast(FP4X4), lhsT_scale=wb_sc[:, g, cols],
                            rhs=x_c["b", mh][:, xs].bitcast(FP8X4), rhs_scale=x_sc["b", mh][:, xs], start=False, stop=True,
                        )
                    ts = slice(t0, t0 + per_bank)
                    nc.vector.tensor_tensor(y[m0, g][:, ts, :], py[:], y[m0, g][:, ts, :], ALU.add)
                nc.sync.dma_start(out=out_y[g, :, :, ms], in_=y[m0, g])
                ybf = kt([PARTS, w, 4], BF16, "ybf%d_%d" % (m0, g))
                interleave(ybf[:], y[m0, g])
                quantize(y_c[:, g, :], y_sc[:, g, ms], ybf[:].rearrange("p m t -> p (m t)"))
            nc.sync.dma_start(out=out_words[:, :, ms], in_=y_c[:].bitcast(I32))
        for q in range(4):
            eng = (nc.sync, nc.scalar)[q % 2]
            eng.dma_start(
                out=out_2[:, 4 * q : 4 * q + 4, :].rearrange("g r m -> r g m").bitcast(I32),
                in_=y_sc[32 * q : 32 * q + 4, :, :].bitcast(I32),
            )
